import numpy as np, ml_dtypes
CORES = [66,74,82,90,194,202,210,218]
N = 8
import mx_ref
NC, WT = 128, 2
LR = np.float32(2.0 ** -2)
BF = ml_dtypes.bfloat16
def cut(t, i, w=512):
    return t[:, w * i:w * i + w]
def tile(rs):
    return np.stack(rs, axis=2).reshape(128, -1).astype(BF)
def pick(b):
    s = np.zeros((128, 128, 4), np.float32)
    s[np.arange(128), np.arange(128), b] = 1.0
    return mx_ref.quantize(s.reshape(128, 512).astype(BF))
def pk(c, s, i=0):
    return (np.ascontiguousarray(c[:, 512 * i:512 * i + 512]), mx_ref.live(s[:, 128 * i:128 * i + 128]))
def inputs(rng, e, E):
    def f(*shape):
        v = (rng.standard_normal(shape, dtype=np.float32) * np.exp2(rng.integers(-2, 3, shape[:-1] + (1,)))).astype(BF)
        return mx_ref.spread((v.astype(np.float32) * np.exp2(rng.integers(-E, E + 1, shape[:-2] + (1, 1))).astype(np.float32)).astype(BF), rng, e)
    def packed(k):
        c = np.zeros((N, 128, k * 512), np.uint8); s = np.zeros((N, 128, k * 128), np.uint8)
        for r in range(N):
            for i in range(k):
                a, b = mx_ref.quantize(f(128, 512)); c[r][:, 512 * i:512 * i + 512] = a; s[r][:, 128 * i:128 * i + 128] = mx_ref.plane(b, rng)
        return c, s
    d = {}
    d["wc"], d["ws"] = packed(WT)
    d["gr"] = f(N, 128, WT * 512)
    d["x"] = f(N, 128, 4 * NC)
    return d
def setup_inputs(rng):
    return inputs(rng, 0, 0)
def setup_inputs_blocks(rng):
    return inputs(rng, 2, 0)
def setup_inputs_wide(rng):
    return inputs(rng, 0, 4)
def setup_inputs_faint(rng):
    d = setup_inputs(rng); d["gr"] = mx_ref.flush((d["gr"].astype(np.float32) * np.float32(2.0 ** -12)).astype(BF))
    return d
def reference(wc, ws, gr, x):
    S = [pick(t) for t in range(4)]
    H = [mx_ref.quantize(tile([mx_ref.matmul(S[t], pk(wc[j], ws[j], i)) - cut(gr[j], i).astype(np.float32)[:, t::4] * LR for t in range(4)])) for j in range(N) for i in range(WT)]
    y = np.zeros((N, 128, N * WT * NC), np.float32)
    for r in range(N):
        X = mx_ref.quantize(x[r])
        for b in range(N * WT):
            y[r][:, NC * b:NC * b + NC] = mx_ref.matmul(H[b], X)
    return {"y": y}

@@ -1,0 +1,181 @@
+from concourse.bass import DstId, RemoteDMATransfer
+from concourse.mybir import dt, AluOpType, ActivationFunctionType
+
+N, WT, NC = 8, 2, 128
+BC = WT * NC
+
+SCRATCH = {
+    "wcs": ("sbuf", [128, BC], "float8_e4m3fn_x4"),
+    "wps": ("sbuf", [128, BC], "uint8"),
+    "gt": ("sbuf", [128, 4 * BC], "bfloat16"),
+    "gs": ("sbuf", [128, 4 * BC], "bfloat16"),
+    "vt": ("sbuf", [128, 4 * BC], "bfloat16"),
+    "xt": ("sbuf", [128, 4 * NC], "bfloat16"),
+    "et": ("sbuf", [128, 4 * NC + 4], "bfloat16"),
+    "em": ("sbuf", [128, 4 * NC + 4], "bfloat16"),
+    "sq": ("sbuf", [128, 4 * NC], "float8_e4m3fn_x4"),
+    "sp": ("sbuf", [128, 4 * NC], "uint8"),
+    "xq": ("sbuf", [128, NC], "float8_e4m3fn_x4"),
+    "xp": ("sbuf", [128, NC], "uint8"),
+    "vq": ("sbuf", [128, N * BC], "float8_e4m3fn_x4"),
+    "vp": ("sbuf", [128, N * BC], "uint8"),
+    "ys": ("sbuf", [128, N * BC], "float32"),
+    "pb": ("psum", [128, 512 * 8], "float32"),
+}
+SEMAPHORES = (["ldw", "ldg0", "ldg1", "ldx", "iot", "eye", "sel", "gsc", "dmm", "sub", "qv", "qx", "mm0", "mm1", "ev0", "ev1",
+               "st", "hp", "hc", "sent"] + ["arr%d" % j for j in range(N)])
+
+
+def _bits(m):
+    return bin(m).count("1")
+
+
+def _plan(s, T, topo):
+    r = T.rank_of(s)
+    away = sorted((j for j in range(N) if j != r), key=lambda j: j ^ r)
+    mate = [j for j in away if topo.mates(s, T.cores[j])][0]
+    P = [j for j in away if topo.same_plane(s, T.cores[j])]
+    Q = [[j for j in away if topo.mates(T.cores[j], T.cores[p])][0] for p in P]
+    free = [c for c in range(256) if c != s and (topo.host(c), topo.chip(c)) == (topo.host(s), topo.chip(s))
+            and all(topo.may_write(c, T.cores[j]) for j in away)]
+    near = [c for c in free if topo.die(c) == topo.die(s)][0]
+    far = [c for c in free if topo.die(c) != topo.die(s)][0]
+    return {"near": near, "far": far,
+            "sends": {s: [P[0], P[1], mate], near: [Q[0], P[2]], far: [Q[1], Q[2]]},
+            "order": [[r], [P[0]], [P[1]], [Q[0]], [Q[1]], [mate], [P[2], Q[2]]]}
+
+
+def _codes(T, j):
+    return T.vq[:, BC * j:BC * j + BC].bitcast(dt.uint8)
+
+
+def _planes(T, j):
+    return T.vp[:, BC * j:BC * j + BC]
+
+
+def _send(g, core, T, topo, view, dests, mask, sem):
+    if len(dests) == 1:
+        rid, pid = topo.addr(dests[0], core)
+        g.remote_dma(out_ap=view, in_ap=view, remote_sem=sem, local_sem=T.sem.sent, pid=pid, routing_id=rid, dma_engine_mask=mask)
+    else:
+        ids = []
+        for d in dests:
+            rid, pid = topo.addr(d, core)
+            ids.append(DstId(rid=rid, pnc=pid))
+        g.remote_dma_fused([RemoteDMATransfer(dst_ids=ids, dma_engine_mask=mask, remote_sem=sem, srcs=[view], dsts=[view for d in dests])],
+                           local_sem=T.sem.sent)
+    return _bits(mask)
+
+
+def _helper(g, core, T, topo, s):
+    r = T.rank_of(s)
+    plan = _plan(s, T, topo)
+    to = [T.cores[j] for j in plan["sends"][core]]
+    feed = _bits(topo.mask(s, core) & ~topo.mask(s, to[0]))
+    mask = topo.mask(core, to[0])
+    arr = T.sem["arr%d" % r]
+    g.wait_ge(T.sem.hp, feed)
+    n = _send(g, core, T, topo, _planes(T, r), to, mask, arr)
+    g.wait_ge(T.sem.hc, feed)
+    for d in to:
+        n += _send(g, core, T, topo, _codes(T, r), [d], mask, arr)
+    g.wait_ge(T.sem.sent, n)
+
+
+def rank_program(g, core, T, topo):
+    rank = T.rank_of(core)
+    if rank is None:
+        for s in T.cores:
+            if (topo.host(s), topo.chip(s)) == (topo.host(core), topo.chip(core)):
+                plan = _plan(s, T, topo)
+                if core in (plan["near"], plan["far"]):
+                    _helper(g, core, T, topo, s)
+        return
+    S = T.sem
+    plan = _plan(core, T, topo)
+    order = [j for grp in plan["order"] for j in grp]
+    W4 = 4 * NC
+
+    g.sync.dma_start(T.wcs[:].bitcast(dt.uint8), T.wc[:]).then_inc(S.ldw, 16)
+    g.scalar.dma_start(T.wps[:], T.ws[:]).then_inc(S.ldw, 16)
+    g.scalar.dma_start(T.gt[:, 0:W4], T.gr[:, 0:W4]).then_inc(S.ldg0, 16)
+    g.sync.dma_start(T.gt[:, W4:2 * W4], T.gr[:, W4:2 * W4]).then_inc(S.ldg1, 16)
+    g.sync.dma_start(T.xt[:], T.x[:]).then_inc(S.ldx, 16)
+
+    g.iota(T.et[:], [[1, W4 + 4]], -3, -4, allow_small_or_imprecise_dtypes=True).then_inc(S.iot, 1)
+    v = g.vector
+    v.wait_ge(S.iot, 1)
+    v.tensor_scalar(T.em[:], T.et[:], 0.0, None, AluOpType.is_equal).then_inc(S.eye, 1)
+    v.wait_ge(S.eye, 1)
+    for b in range(4):
+        v.quantize_mx(T.sq[:, NC * b:NC * b + NC], T.sp[:, NC * b:NC * b + NC], T.em[:, 3 - b:3 - b + W4]).then_inc(S.sel, 1)
+
+    t = g.tensor
+    t.wait_ge(S.sel, 4)
+    t.wait_ge(S.ldw, 32)
+    for b in range(4):
+        t.matmul_mx(T.pb[:, 512 * b:512 * b + BC], T.sq[:, NC * b:NC * b + NC], T.sp[:, NC * b:NC * b + NC],
+                    T.wcs[:], T.wps[:], True, True).then_inc(S.dmm, 1)
+
+    for i in range(WT):
+        o = W4 * i
+        v.wait_ge(S["ldg%d" % i] if False else T.sem["ldg%d" % i], 16)
+        v.tensor_scalar(T.gs[:, o:o + W4], T.gt[:, o:o + W4], 0.25, None, AluOpType.mult).then_inc(S.gsc, 1)
+        v.wait_ge(S.gsc, i + 1)
+        for b in range(4):
+            if i == 0:
+                v.wait_ge(S.dmm, b + 1)
+            v.tensor_tensor(T.vt[:, o + b:o + W4:4], T.pb[:, 512 * b + NC * i:512 * b + NC * i + NC], T.gs[:, o + b:o + W4:4],
+                            AluOpType.subtract).then_inc(S.sub, 1)
+        v.wait_ge(S.sub, 4 * (i + 1))
+        k = BC * rank + NC * i
+        v.quantize_mx(T.vq[:, k:k + NC], T.vp[:, k:k + NC], T.vt[:, o:o + W4]).then_inc(S.qv, 1)
+    v.wait_ge(S.ldx, 16)
+    v.quantize_mx(T.xq[:], T.xp[:], T.xt[:]).then_inc(S.qx, 1)
+
+    mine = [T.cores[j] for j in plan["sends"][core]]
+    off = topo.mask(core, mine[0])
+    feed = topo.mask(core, plan["near"]) & topo.mask(core, plan["far"]) & ~off
+    helpers = [plan["near"], plan["far"]]
+    arr = T.sem["arr%d" % rank]
+    g.wait_ge(S.qv, WT)
+    n = _send(g, core, T, topo, _planes(T, rank), helpers, feed, S.hp)
+    n += _send(g, core, T, topo, _codes(T, rank), helpers, feed, S.hc)
+    for d in mine:
+        n += _send(g, core, T, topo, _planes(T, rank), [d], off, arr)
+        n += _send(g, core, T, topo, _codes(T, rank), [d], off, arr)
+    g.wait_ge(S.sent, n)
+
+    t.wait_ge(S.qv, WT)
+    t.wait_ge(S.qx, 1)
+    landed = 2 * _bits(off)
+    for i, j in enumerate(order):
+        if j != rank:
+            t.wait_ge(T.sem["arr%d" % j], landed)
+        if i >= 4:
+            t.wait_ge(S.ev0, i - 3)
+            t.wait_ge(S.ev1, i - 3)
+        for h in range(WT):
+            bank = (4 + 2 * i + h) % 8
+            k = BC * j + NC * h
+            t.matmul_mx(T.pb[:, 512 * bank:512 * bank + NC], T.vq[:, k:k + NC], T.vp[:, k:k + NC], T.xq[:], T.xp[:],
+                        True, True).then_inc(T.sem["mm%d" % h], 1)
+    for i, j in enumerate(order):
+        b0, b1 = 512 * ((4 + 2 * i) % 8), 512 * ((5 + 2 * i) % 8)
+        k = BC * j
+        v.wait_ge(S.mm0, i + 1)
+        v.tensor_copy(T.ys[:, k:k + NC], T.pb[:, b0:b0 + NC]).then_inc(S.ev0, 1)
+        g.scalar.wait_ge(S.mm1, i + 1)
+        g.scalar.activation(T.ys[:, k + NC:k + BC], T.pb[:, b1:b1 + NC], ActivationFunctionType.Copy).then_inc(S.ev1, 1)
+
+    done = stores = 0
+    for grp in plan["order"]:
+        lo, hi = min(grp), max(grp) + 1
+        runs = [(lo, hi)] if hi - lo == len(grp) else [(j, j + 1) for j in grp]
+        done += len(grp)
+        g.sync.wait_ge(S.ev0, done)
+        g.sync.wait_ge(S.ev1, done)
+        for a, b in runs:
+            g.sync.dma_start(T.y[:, BC * a:BC * b], T.ys[:, BC * a:BC * b]).then_inc(S.st, 16)
+            stores += 1
+    g.sync.wait_ge(S.st, 16 * stores)

@@ -22,8 +22,8 @@ SCRATCH = {
     "ys": ("sbuf", [128, N * BC], "float32"),
     "pb": ("psum", [128, 512 * 8], "float32"),
 }
-SEMAPHORES = (["ldw", "ldg0", "ldg1", "ldx", "iot", "eye", "sel", "gsc", "dmm", "sub", "qv", "qx", "mm0", "mm1", "ev0", "ev1",
-               "st", "hp", "hc", "sent"] + ["arr%d" % j for j in range(N)])
+SEMAPHORES = (["ldw", "ldg0", "ldg1", "ldx", "iot", "eye", "sel", "dmm", "sub0", "sub1", "gsc0", "gsc1", "qv", "qx",
+               "mm0", "mm1", "ev0", "ev1", "st", "hp", "hc", "sent"] + ["arr%d" % j for j in range(N)])
 
 
 def _bits(m):
@@ -36,49 +36,50 @@ def _plan(s, T, topo):
     mate = [j for j in away if topo.mates(s, T.cores[j])][0]
     P = [j for j in away if topo.same_plane(s, T.cores[j])]
     Q = [[j for j in away if topo.mates(T.cores[j], T.cores[p])][0] for p in P]
-    free = [c for c in range(256) if c != s and (topo.host(c), topo.chip(c)) == (topo.host(s), topo.chip(s))
-            and all(topo.may_write(c, T.cores[j]) for j in away)]
-    near = [c for c in free if topo.die(c) == topo.die(s)][0]
-    far = [c for c in free if topo.die(c) != topo.die(s)][0]
-    return {"near": near, "far": far,
-            "sends": {s: [P[0], P[1], mate], near: [Q[0], P[2]], far: [Q[1], Q[2]]},
-            "order": [[r], [P[0]], [P[1]], [Q[0]], [Q[1]], [mate], [P[2], Q[2]]]}
+    far = [c for c in range(256) if (topo.host(c), topo.chip(c)) == (topo.host(s), topo.chip(s))
+           and topo.die(c) != topo.die(s) and all(topo.may_write(c, T.cores[j]) for j in away)][:2]
+    return {"helpers": far, "first": P[0],
+            "sends": {s: [P[0], Q[2], Q[1]], far[0]: [Q[0], mate], far[1]: [P[1], P[2]]},
+            "order": [r, P[0], Q[2], Q[1], Q[0], P[1], mate, P[2]]}
 
 
-def _codes(T, j):
-    return T.vq[:, BC * j:BC * j + BC].bitcast(dt.uint8)
+def _codes(T, j, a=0, b=BC):
+    return T.vq[:, BC * j + a:BC * j + b].bitcast(dt.uint8)
 
 
 def _planes(T, j):
     return T.vp[:, BC * j:BC * j + BC]
 
 
-def _send(g, core, T, topo, view, dests, mask, sem):
-    if len(dests) == 1:
-        rid, pid = topo.addr(dests[0], core)
+def _send(g, core, T, topo, view, *ways):
+    if len(ways) == 1 and len(ways[0][0]) == 1:
+        (d,), mask, sem = ways[0]
+        rid, pid = topo.addr(d, core)
         g.remote_dma(out_ap=view, in_ap=view, remote_sem=sem, local_sem=T.sem.sent, pid=pid, routing_id=rid, dma_engine_mask=mask)
-    else:
+        return _bits(mask)
+    moves = []
+    for dests, mask, sem in ways:
         ids = []
         for d in dests:
             rid, pid = topo.addr(d, core)
             ids.append(DstId(rid=rid, pnc=pid))
-        g.remote_dma_fused([RemoteDMATransfer(dst_ids=ids, dma_engine_mask=mask, remote_sem=sem, srcs=[view], dsts=[view for d in dests])],
-                           local_sem=T.sem.sent)
-    return _bits(mask)
+        moves.append(RemoteDMATransfer(dst_ids=ids, dma_engine_mask=mask, remote_sem=sem, srcs=[view], dsts=[view for d in dests]))
+    g.remote_dma_fused(moves, local_sem=T.sem.sent)
+    return sum(_bits(w[1]) for w in ways)
 
 
 def _helper(g, core, T, topo, s):
     r = T.rank_of(s)
     plan = _plan(s, T, topo)
     to = [T.cores[j] for j in plan["sends"][core]]
-    feed = _bits(topo.mask(s, core) & ~topo.mask(s, to[0]))
     mask = topo.mask(core, to[0])
+    feed = _bits(topo.mask(s, core) & ~topo.mask(s, to[0]))
     arr = T.sem["arr%d" % r]
     g.wait_ge(T.sem.hp, feed)
-    n = _send(g, core, T, topo, _planes(T, r), to, mask, arr)
-    g.wait_ge(T.sem.hc, feed)
+    n = _send(g, core, T, topo, _planes(T, r), (to, mask, arr))
+    g.wait_ge(T.sem.hc, WT * feed)
     for d in to:
-        n += _send(g, core, T, topo, _codes(T, r), [d], mask, arr)
+        n += _send(g, core, T, topo, _codes(T, r), ([d], mask, arr))
     g.wait_ge(T.sem.sent, n)
 
 
@@ -87,18 +88,17 @@ def rank_program(g, core, T, topo):
     if rank is None:
         for s in T.cores:
             if (topo.host(s), topo.chip(s)) == (topo.host(core), topo.chip(core)):
-                plan = _plan(s, T, topo)
-                if core in (plan["near"], plan["far"]):
+                if core in _plan(s, T, topo)["helpers"]:
                     _helper(g, core, T, topo, s)
         return
     S = T.sem
     plan = _plan(core, T, topo)
-    order = [j for grp in plan["order"] for j in grp]
+    order = plan["order"]
     W4 = 4 * NC
 
     g.sync.dma_start(T.wcs[:].bitcast(dt.uint8), T.wc[:]).then_inc(S.ldw, 16)
-    g.scalar.dma_start(T.wps[:], T.ws[:]).then_inc(S.ldw, 16)
     g.scalar.dma_start(T.gt[:, 0:W4], T.gr[:, 0:W4]).then_inc(S.ldg0, 16)
+    g.scalar.dma_start(T.wps[:], T.ws[:]).then_inc(S.ldw, 16)
     g.sync.dma_start(T.gt[:, W4:2 * W4], T.gr[:, W4:2 * W4]).then_inc(S.ldg1, 16)
     g.sync.dma_start(T.xt[:], T.x[:]).then_inc(S.ldx, 16)
 
@@ -113,69 +113,72 @@ def rank_program(g, core, T, topo):
     t = g.tensor
     t.wait_ge(S.sel, 4)
     t.wait_ge(S.ldw, 32)
-    for b in range(4):
-        t.matmul_mx(T.pb[:, 512 * b:512 * b + BC], T.sq[:, NC * b:NC * b + NC], T.sp[:, NC * b:NC * b + NC],
-                    T.wcs[:], T.wps[:], True, True).then_inc(S.dmm, 1)
+    for i in range(WT):
+        for b in range(4):
+            k = 512 * (4 * i + b)
+            t.matmul_mx(T.pb[:, k:k + NC], T.sq[:, NC * b:NC * b + NC], T.sp[:, NC * b:NC * b + NC],
+                        T.wcs[:, NC * i:NC * i + NC], T.wps[:, NC * i:NC * i + NC], True, True).then_inc(S.dmm, 1)
 
+    g.scalar.wait_ge(S.ldg1, 16)
+    g.scalar.activation(T.gs[:, W4:2 * W4], T.gt[:, W4:2 * W4], ActivationFunctionType.Copy, scale=0.25).then_inc(S.gsc1, 1)
+    v.wait_ge(S.ldg0, 16)
+    v.tensor_scalar(T.gs[:, 0:W4], T.gt[:, 0:W4], 0.25, None, AluOpType.mult).then_inc(S.gsc0, 1)
     for i in range(WT):
         o = W4 * i
-        v.wait_ge(S["ldg%d" % i] if False else T.sem["ldg%d" % i], 16)
-        v.tensor_scalar(T.gs[:, o:o + W4], T.gt[:, o:o + W4], 0.25, None, AluOpType.mult).then_inc(S.gsc, 1)
-        v.wait_ge(S.gsc, i + 1)
+        v.wait_ge(T.sem["gsc%d" % i], 1)
         for b in range(4):
-            if i == 0:
-                v.wait_ge(S.dmm, b + 1)
-            v.tensor_tensor(T.vt[:, o + b:o + W4:4], T.pb[:, 512 * b + NC * i:512 * b + NC * i + NC], T.gs[:, o + b:o + W4:4],
-                            AluOpType.subtract).then_inc(S.sub, 1)
-        v.wait_ge(S.sub, 4 * (i + 1))
+            k = 512 * (4 * i + b)
+            v.wait_ge(S.dmm, 4 * i + b + 1)
+            v.tensor_tensor(T.vt[:, o + b:o + W4:4], T.pb[:, k:k + NC], T.gs[:, o + b:o + W4:4],
+                            AluOpType.subtract).then_inc(T.sem["sub%d" % i], 1)
+        v.wait_ge(T.sem["sub%d" % i], 4)
         k = BC * rank + NC * i
         v.quantize_mx(T.vq[:, k:k + NC], T.vp[:, k:k + NC], T.vt[:, o:o + W4]).then_inc(S.qv, 1)
     v.wait_ge(S.ldx, 16)
     v.quantize_mx(T.xq[:], T.xp[:], T.xt[:]).then_inc(S.qx, 1)
 
     mine = [T.cores[j] for j in plan["sends"][core]]
+    helpers = plan["helpers"]
     off = topo.mask(core, mine[0])
-    feed = topo.mask(core, plan["near"]) & topo.mask(core, plan["far"]) & ~off
-    helpers = [plan["near"], plan["far"]]
+    feed = topo.mask(core, helpers[0]) & ~off
     arr = T.sem["arr%d" % rank]
+    g.wait_ge(S.qv, 1)
+    n = _send(g, core, T, topo, _codes(T, rank, 0, NC), (helpers, feed, S.hc), (mine[:1], off, arr))
     g.wait_ge(S.qv, WT)
-    n = _send(g, core, T, topo, _planes(T, rank), helpers, feed, S.hp)
-    n += _send(g, core, T, topo, _codes(T, rank), helpers, feed, S.hc)
-    for d in mine:
-        n += _send(g, core, T, topo, _planes(T, rank), [d], off, arr)
-        n += _send(g, core, T, topo, _codes(T, rank), [d], off, arr)
+    n += _send(g, core, T, topo, _planes(T, rank), (helpers, feed, S.hp), (mine[:1], off, arr))
+    n += _send(g, core, T, topo, _codes(T, rank, NC, BC), (helpers, feed, S.hc), (mine[:1], off, arr))
+    n += _send(g, core, T, topo, _planes(T, rank), (mine[1:], off, arr))
+    for d in mine[1:]:
+        n += _send(g, core, T, topo, _codes(T, rank), ([d], off, arr))
     g.wait_ge(S.sent, n)
 
     t.wait_ge(S.qv, WT)
     t.wait_ge(S.qx, 1)
-    landed = 2 * _bits(off)
+    landed = {j: 2 * _bits(off) for j in order}
+    for j in order:
+        if j != rank and _plan(T.cores[j], T, topo)["first"] == rank:
+            landed[j] = 3 * _bits(off)
     for i, j in enumerate(order):
         if j != rank:
-            t.wait_ge(T.sem["arr%d" % j], landed)
+            t.wait_ge(T.sem["arr%d" % j], landed[j])
         if i >= 4:
             t.wait_ge(S.ev0, i - 3)
             t.wait_ge(S.ev1, i - 3)
         for h in range(WT):
-            bank = (4 + 2 * i + h) % 8
+            bank = (2 * i + h) % 8
             k = BC * j + NC * h
             t.matmul_mx(T.pb[:, 512 * bank:512 * bank + NC], T.vq[:, k:k + NC], T.vp[:, k:k + NC], T.xq[:], T.xp[:],
                         True, True).then_inc(T.sem["mm%d" % h], 1)
     for i, j in enumerate(order):
-        b0, b1 = 512 * ((4 + 2 * i) % 8), 512 * ((5 + 2 * i) % 8)
+        b0, b1 = 512 * (2 * i % 8), 512 * ((2 * i + 1) % 8)
         k = BC * j
         v.wait_ge(S.mm0, i + 1)
         v.tensor_copy(T.ys[:, k:k + NC], T.pb[:, b0:b0 + NC]).then_inc(S.ev0, 1)
         g.scalar.wait_ge(S.mm1, i + 1)
         g.scalar.activation(T.ys[:, k + NC:k + BC], T.pb[:, b1:b1 + NC], ActivationFunctionType.Copy).then_inc(S.ev1, 1)
 
-    done = stores = 0
-    for grp in plan["order"]:
-        lo, hi = min(grp), max(grp) + 1
-        runs = [(lo, hi)] if hi - lo == len(grp) else [(j, j + 1) for j in grp]
-        done += len(grp)
-        g.sync.wait_ge(S.ev0, done)
-        g.sync.wait_ge(S.ev1, done)
-        for a, b in runs:
-            g.sync.dma_start(T.y[:, BC * a:BC * b], T.ys[:, BC * a:BC * b]).then_inc(S.st, 16)
-            stores += 1
-    g.sync.wait_ge(S.st, 16 * stores)
+    for i, j in enumerate(order):
+        g.sync.wait_ge(S.ev0, i + 1)
+        g.sync.wait_ge(S.ev1, i + 1)
+        g.sync.dma_start(T.y[:, BC * j:BC * j + BC], T.ys[:, BC * j:BC * j + BC]).then_inc(S.st, 16)
+    g.sync.wait_ge(S.st, 16 * N)

@@ -3,6 +3,17 @@ from concourse.mybir import dt, AluOpType, ActivationFunctionType
 
 N, WT, NC = 8, 2, 128
 BC = WT * NC
+W4 = 4 * NC
+
+HELP = {
+    "far0": [("c0", ["Q0"]), ("p", ["Q0"]), ("c1", ["Q0"])],
+    "far1": [("c0", ["P1"]), ("p", ["P1", "P0"]), ("c1", ["P1"]), ("c", ["P0"])],
+    "near": [("c0", ["P2"]), ("p", ["P2"]), ("c1", ["P2"])],
+}
+HELPERS = ["far0", "far1", "near"]
+OWN = [("c0", True, []), ("p", True, ["Q1"]), ("c1", True, []), ("c", False, ["Q1"]),
+       ("p", False, ["Q2", "M"]), ("c", False, ["Q2"]), ("c", False, ["M"])]
+ORDER = ["S", "Q1", "Q2", "M", "Q0", "P1", "P2", "P0"]
 
 SCRATCH = {
     "wcs": ("sbuf", [128, BC], "float8_e4m3fn_x4"),
@@ -10,11 +21,11 @@ SCRATCH = {
     "gt": ("sbuf", [128, 4 * BC], "bfloat16"),
     "gs": ("sbuf", [128, 4 * BC], "bfloat16"),
     "vt": ("sbuf", [128, 4 * BC], "bfloat16"),
-    "xt": ("sbuf", [128, 4 * NC], "bfloat16"),
-    "et": ("sbuf", [128, 4 * NC + 4], "bfloat16"),
-    "em": ("sbuf", [128, 4 * NC + 4], "bfloat16"),
-    "sq": ("sbuf", [128, 4 * NC], "float8_e4m3fn_x4"),
-    "sp": ("sbuf", [128, 4 * NC], "uint8"),
+    "xt": ("sbuf", [128, W4], "bfloat16"),
+    "et": ("sbuf", [128, NC], "bfloat16"),
+    "em": ("sbuf", [128, W4 + 4], "bfloat16"),
+    "sq": ("sbuf", [128, W4], "float8_e4m3fn_x4"),
+    "sp": ("sbuf", [128, W4], "uint8"),
     "xq": ("sbuf", [128, NC], "float8_e4m3fn_x4"),
     "xp": ("sbuf", [128, NC], "uint8"),
     "vq": ("sbuf", [128, N * BC], "float8_e4m3fn_x4"),
@@ -22,33 +33,39 @@ SCRATCH = {
     "ys": ("sbuf", [128, N * BC], "float32"),
     "pb": ("psum", [128, 512 * 8], "float32"),
 }
-SEMAPHORES = (["ldw", "ldg0", "ldg1", "ldx", "iot", "eye", "sel", "dmm", "sub0", "sub1", "gsc0", "gsc1", "qv", "qx",
-               "mm0", "mm1", "ev0", "ev1", "st", "hp", "hc", "sent"] + ["arr%d" % j for j in range(N)])
+SEMAPHORES = (["ldw0", "ldw1", "ldg0", "ldg1", "ldx", "zer", "iot", "eye", "sel", "dmm", "gsv", "gsc", "sub0", "sub1", "qv", "qx",
+               "mm0", "mm1", "ev0", "ev1", "st", "hc0", "hc1", "hp", "sent"] + ["arr%d" % j for j in range(N)])
 
 
 def _bits(m):
     return bin(m).count("1")
 
 
-def _plan(s, T, topo):
+def _roles(s, T, topo):
     r = T.rank_of(s)
     away = sorted((j for j in range(N) if j != r), key=lambda j: j ^ r)
-    mate = [j for j in away if topo.mates(s, T.cores[j])][0]
-    P = [j for j in away if topo.same_plane(s, T.cores[j])]
-    Q = [[j for j in away if topo.mates(T.cores[j], T.cores[p])][0] for p in P]
-    far = [c for c in range(256) if (topo.host(c), topo.chip(c)) == (topo.host(s), topo.chip(s))
-           and topo.die(c) != topo.die(s) and all(topo.may_write(c, T.cores[j]) for j in away)][:2]
-    return {"helpers": far, "first": P[0],
-            "sends": {s: [P[0], Q[2], Q[1]], far[0]: [Q[0], mate], far[1]: [P[1], P[2]]},
-            "order": [r, P[0], Q[2], Q[1], Q[0], P[1], mate, P[2]]}
+    who = {"S": s, "M": [T.cores[j] for j in away if topo.mates(s, T.cores[j])][0]}
+    for i, p in enumerate(T.cores[j] for j in away if topo.same_plane(s, T.cores[j])):
+        who["P%d" % i] = p
+        who["Q%d" % i] = [T.cores[j] for j in away if topo.mates(T.cores[j], p)][0]
+    able = [c for c in range(256) if c != s and (topo.host(c), topo.chip(c)) == (topo.host(s), topo.chip(s))
+            and all(topo.may_write(c, T.cores[j]) for j in away)]
+    who["far0"], who["far1"] = [c for c in able if topo.die(c) != topo.die(s)][:2]
+    who["near"] = [c for c in able if topo.die(c) == topo.die(s)][0]
+    return who
 
 
-def _codes(T, j, a=0, b=BC):
-    return T.vq[:, BC * j + a:BC * j + b].bitcast(dt.uint8)
+def _masks(topo, who):
+    off = topo.mask(who["S"], who["M"])
+    return off, topo.mask(who["S"], who["near"]) & ~off
 
 
-def _planes(T, j):
-    return T.vp[:, BC * j:BC * j + BC]
+def _view(T, r, piece):
+    k = BC * r
+    if piece == "p":
+        return T.vp[:, k:k + BC]
+    a, b = {"c": (0, BC), "c0": (0, NC), "c1": (NC, BC)}[piece]
+    return T.vq[:, k + a:k + b].bitcast(dt.uint8)
 
 
 def _send(g, core, T, topo, view, *ways):
@@ -68,18 +85,21 @@ def _send(g, core, T, topo, view, *ways):
     return sum(_bits(w[1]) for w in ways)
 
 
-def _helper(g, core, T, topo, s):
+def _writes(name):
+    return (sum(name in dests for piece, feed, dests in OWN)
+            + sum(name in dests for h in HELPERS for piece, dests in HELP[h]))
+
+
+def _helper(g, core, T, topo, s, who, name):
     r = T.rank_of(s)
-    plan = _plan(s, T, topo)
-    to = [T.cores[j] for j in plan["sends"][core]]
-    mask = topo.mask(core, to[0])
-    feed = _bits(topo.mask(s, core) & ~topo.mask(s, to[0]))
-    arr = T.sem["arr%d" % r]
-    g.wait_ge(T.sem.hp, feed)
-    n = _send(g, core, T, topo, _planes(T, r), (to, mask, arr))
-    g.wait_ge(T.sem.hc, WT * feed)
-    for d in to:
-        n += _send(g, core, T, topo, _codes(T, r), ([d], mask, arr))
+    off, on = _masks(topo, who)
+    n, seen = 0, []
+    for piece, dests in HELP[name]:
+        for q in ["c0", "c1"] if piece == "c" else [piece]:
+            if q not in seen:
+                seen.append(q)
+                g.wait_ge(T.sem["h" + q], _bits(on))
+        n += _send(g, core, T, topo, _view(T, r, piece), ([who[d] for d in dests], off, T.sem["arr%d" % r]))
     g.wait_ge(T.sem.sent, n)
 
 
@@ -88,48 +108,61 @@ def rank_program(g, core, T, topo):
     if rank is None:
         for s in T.cores:
             if (topo.host(s), topo.chip(s)) == (topo.host(core), topo.chip(core)):
-                if core in _plan(s, T, topo)["helpers"]:
-                    _helper(g, core, T, topo, s)
+                who = _roles(s, T, topo)
+                for name in HELPERS:
+                    if who[name] == core:
+                        _helper(g, core, T, topo, s, who, name)
         return
     S = T.sem
-    plan = _plan(core, T, topo)
-    order = plan["order"]
-    W4 = 4 * NC
+    v, t, sc, sy = g.vector, g.tensor, g.scalar, g.sync
+    who = _roles(core, T, topo)
+    order = [T.rank_of(who[n]) for n in ORDER]
 
-    g.sync.dma_start(T.wcs[:].bitcast(dt.uint8), T.wc[:]).then_inc(S.ldw, 16)
-    g.scalar.dma_start(T.gt[:, 0:W4], T.gr[:, 0:W4]).then_inc(S.ldg0, 16)
-    g.scalar.dma_start(T.wps[:], T.ws[:]).then_inc(S.ldw, 16)
-    g.sync.dma_start(T.gt[:, W4:2 * W4], T.gr[:, W4:2 * W4]).then_inc(S.ldg1, 16)
-    g.sync.dma_start(T.xt[:], T.x[:]).then_inc(S.ldx, 16)
+    sy.dma_start(T.wcs[:, 0:NC].bitcast(dt.uint8), T.wc[:, 0:W4]).then_inc(S.ldw0, 16)
+    sc.dma_start(T.wps[:], T.ws[:]).then_inc(S.ldw0, 16)
+    sc.dma_start(T.gt[:, 0:W4], T.gr[:, 0:W4]).then_inc(S.ldg0, 16)
+    sy.dma_start(T.wcs[:, NC:BC].bitcast(dt.uint8), T.wc[:, W4:2 * W4]).then_inc(S.ldw1, 16)
+    sy.dma_start(T.gt[:, W4:2 * W4], T.gr[:, W4:2 * W4]).then_inc(S.ldg1, 16)
+    sy.wait_ge(S.ldg0, 16)
+    sy.dma_start(T.xt[:], T.x[:]).then_inc(S.ldx, 16)
 
-    g.iota(T.et[:], [[1, W4 + 4]], -3, -4, allow_small_or_imprecise_dtypes=True).then_inc(S.iot, 1)
-    v = g.vector
+    v.memset(T.em[:], 0.0).then_inc(S.zer, 1)
+    g.iota(T.et[:], [[1, NC]], 0, -1, allow_small_or_imprecise_dtypes=True).then_inc(S.iot, 1)
     v.wait_ge(S.iot, 1)
-    v.tensor_scalar(T.em[:], T.et[:], 0.0, None, AluOpType.is_equal).then_inc(S.eye, 1)
+    v.wait_ge(S.zer, 1)
+    v.tensor_scalar(T.em[:, 3:W4 + 3:4], T.et[:], 0.0, None, AluOpType.is_equal).then_inc(S.eye, 1)
     v.wait_ge(S.eye, 1)
     for b in range(4):
         v.quantize_mx(T.sq[:, NC * b:NC * b + NC], T.sp[:, NC * b:NC * b + NC], T.em[:, 3 - b:3 - b + W4]).then_inc(S.sel, 1)
 
-    t = g.tensor
-    t.wait_ge(S.sel, 4)
-    t.wait_ge(S.ldw, 32)
     for i in range(WT):
+        t.wait_ge(T.sem["ldw%d" % i], 16 * (WT - i))
         for b in range(4):
+            if i == 0:
+                t.wait_ge(S.sel, b + 1)
             k = 512 * (4 * i + b)
             t.matmul_mx(T.pb[:, k:k + NC], T.sq[:, NC * b:NC * b + NC], T.sp[:, NC * b:NC * b + NC],
                         T.wcs[:, NC * i:NC * i + NC], T.wps[:, NC * i:NC * i + NC], True, True).then_inc(S.dmm, 1)
 
-    g.scalar.wait_ge(S.ldg1, 16)
-    g.scalar.activation(T.gs[:, W4:2 * W4], T.gt[:, W4:2 * W4], ActivationFunctionType.Copy, scale=0.25).then_inc(S.gsc1, 1)
     v.wait_ge(S.ldg0, 16)
-    v.tensor_scalar(T.gs[:, 0:W4], T.gt[:, 0:W4], 0.25, None, AluOpType.mult).then_inc(S.gsc0, 1)
+    v.tensor_scalar(T.gs[:, 0:NC], T.gt[:, 0:W4:4], 0.25, None, AluOpType.mult).then_inc(S.gsv, 1)
+    for i in range(WT):
+        sc.wait_ge(T.sem["ldg%d" % i], 16)
+        for b in range(1 - i, 4):
+            k = W4 * i
+            sc.activation(T.gs[:, k + NC * b:k + NC * b + NC], T.gt[:, k + b:k + W4:4], ActivationFunctionType.Copy,
+                          scale=0.25).then_inc(S.gsc, 1)
+
     for i in range(WT):
         o = W4 * i
-        v.wait_ge(T.sem["gsc%d" % i], 1)
         for b in range(4):
             k = 512 * (4 * i + b)
+            if i == b == 0:
+                v.wait_ge(S.gsv, 1)
+            else:
+                v.wait_ge(S.gsc, 4 * i + b)
             v.wait_ge(S.dmm, 4 * i + b + 1)
-            v.tensor_tensor(T.vt[:, o + b:o + W4:4], T.pb[:, k:k + NC], T.gs[:, o + b:o + W4:4],
+            v.tensor_tensor(T.vt[:, o + b:o + W4:4], T.pb[:, k:k + NC], T.gs[:, o + NC * b:o + NC * b + NC],
                             AluOpType.subtract).then_inc(T.sem["sub%d" % i], 1)
         v.wait_ge(T.sem["sub%d" % i], 4)
         k = BC * rank + NC * i
@@ -137,30 +170,25 @@ def rank_program(g, core, T, topo):
     v.wait_ge(S.ldx, 16)
     v.quantize_mx(T.xq[:], T.xp[:], T.xt[:]).then_inc(S.qx, 1)
 
-    mine = [T.cores[j] for j in plan["sends"][core]]
-    helpers = plan["helpers"]
-    off = topo.mask(core, mine[0])
-    feed = topo.mask(core, helpers[0]) & ~off
+    off, on = _masks(topo, who)
     arr = T.sem["arr%d" % rank]
-    g.wait_ge(S.qv, 1)
-    n = _send(g, core, T, topo, _codes(T, rank, 0, NC), (helpers, feed, S.hc), (mine[:1], off, arr))
-    g.wait_ge(S.qv, WT)
-    n += _send(g, core, T, topo, _planes(T, rank), (helpers, feed, S.hp), (mine[:1], off, arr))
-    n += _send(g, core, T, topo, _codes(T, rank, NC, BC), (helpers, feed, S.hc), (mine[:1], off, arr))
-    n += _send(g, core, T, topo, _planes(T, rank), (mine[1:], off, arr))
-    for d in mine[1:]:
-        n += _send(g, core, T, topo, _codes(T, rank), ([d], off, arr))
+    n, made = 0, 0
+    for piece, feed, dests in OWN:
+        need = 1 if piece == "c0" else WT
+        if need > made:
+            g.wait_ge(S.qv, need)
+            made = need
+        ways = [([who[h] for h in HELPERS], on, T.sem["h" + piece])] if feed else []
+        if dests:
+            ways.append(([who[d] for d in dests], off, arr))
+        n += _send(g, core, T, topo, _view(T, rank, piece), *ways)
     g.wait_ge(S.sent, n)
 
     t.wait_ge(S.qv, WT)
     t.wait_ge(S.qx, 1)
-    landed = {j: 2 * _bits(off) for j in order}
-    for j in order:
-        if j != rank and _plan(T.cores[j], T, topo)["first"] == rank:
-            landed[j] = 3 * _bits(off)
     for i, j in enumerate(order):
         if j != rank:
-            t.wait_ge(T.sem["arr%d" % j], landed[j])
+            t.wait_ge(T.sem["arr%d" % j], _bits(off) * _writes(ORDER[i]))
         if i >= 4:
             t.wait_ge(S.ev0, i - 3)
             t.wait_ge(S.ev1, i - 3)
@@ -174,11 +202,17 @@ def rank_program(g, core, T, topo):
         k = BC * j
         v.wait_ge(S.mm0, i + 1)
         v.tensor_copy(T.ys[:, k:k + NC], T.pb[:, b0:b0 + NC]).then_inc(S.ev0, 1)
-        g.scalar.wait_ge(S.mm1, i + 1)
-        g.scalar.activation(T.ys[:, k + NC:k + BC], T.pb[:, b1:b1 + NC], ActivationFunctionType.Copy).then_inc(S.ev1, 1)
+        sc.wait_ge(S.mm1, i + 1)
+        sc.activation(T.ys[:, k + NC:k + BC], T.pb[:, b1:b1 + NC], ActivationFunctionType.Copy).then_inc(S.ev1, 1)
 
-    for i, j in enumerate(order):
-        g.sync.wait_ge(S.ev0, i + 1)
-        g.sync.wait_ge(S.ev1, i + 1)
-        g.sync.dma_start(T.y[:, BC * j:BC * j + BC], T.ys[:, BC * j:BC * j + BC]).then_inc(S.st, 16)
-    g.sync.wait_ge(S.st, 16 * N)
+    for i in [1, 0] + list(range(2, N - 1)):
+        k = BC * order[i]
+        sy.wait_ge(S.ev0, i + 1)
+        sy.wait_ge(S.ev1, i + 1)
+        sy.dma_start(T.y[:, k:k + BC], T.ys[:, k:k + BC]).then_inc(S.st, 16)
+    k = BC * order[N - 1]
+    sy.wait_ge(S.ev0, N)
+    sy.dma_start(T.y[:, k:k + NC], T.ys[:, k:k + NC]).then_inc(S.st, 16)
+    sc.wait_ge(S.ev1, N)
+    sc.dma_start(T.y[:, k + NC:k + BC], T.ys[:, k + NC:k + BC]).then_inc(S.st, 16)
+    sy.wait_ge(S.st, 16 * (N + 1))

@@ -4,16 +4,19 @@ from concourse.mybir import dt, AluOpType, ActivationFunctionType
 N, WT, NC = 8, 2, 128
 BC = WT * NC
 W4 = 4 * NC
+PIECES = {"c": (0, BC), "c0": (0, NC), "c1": (NC, BC), "p": (0, BC), "p0": (0, NC), "p1": (NC, BC)}
 
 HELP = {
-    "far0": [("c0", ["Q0"]), ("p", ["Q0"]), ("c1", ["Q0"])],
-    "far1": [("c0", ["P1"]), ("p", ["P1", "P0"]), ("c1", ["P1"]), ("c", ["P0"])],
-    "near": [("c0", ["P2"]), ("p", ["P2"]), ("c1", ["P2"])],
+    "t0": [("c0", ["Q0", "Q1", "P1"]), ("p1", ["Q1", "P1"])],
+    "t1": [("p0", ["Q1", "P1"]), ("c1", ["Q1", "P1"])],
+    "u0": [("c0", ["P2", "P0"]), ("p1", ["P2", "P0"])],
+    "u1": [("p0", ["P2", "P0"]), ("c1", ["P2", "P0"])],
 }
-HELPERS = ["far0", "far1", "near"]
-OWN = [("c0", True, []), ("p", True, ["Q1"]), ("c1", True, []), ("c", False, ["Q1"]),
-       ("p", False, ["Q2", "M"]), ("c", False, ["Q2"]), ("c", False, ["M"])]
-ORDER = ["S", "Q1", "Q2", "M", "Q0", "P1", "P2", "P0"]
+OWN = [("c0", ["t0", "u0"], []), ("p0", ["t1", "u1"], []), ("c", [], ["Q2"]), ("c1", ["t1", "u1"], ["Q0"]),
+       ("p", [], ["Q2", "Q0", "M"]), ("p1", ["t0", "u0"], []), ("c0", [], ["M"]), ("c1", [], ["M"])]
+UNITS = [("S", 0), ("S", 1), ("Q2", 0), ("Q2", 1), ("Q0", 1), ("Q0", 0), ("M", 0), ("P2", 0), ("Q1", 0), ("M", 1), ("P0", 0), ("P1", 0),
+         ("P2", 1), ("Q1", 1), ("P0", 1), ("P1", 1)]
+WHOLE = ["Q2", "S"]
 
 SCRATCH = {
     "wcs": ("sbuf", [128, BC], "float8_e4m3fn_x4"),
@@ -34,11 +37,16 @@ SCRATCH = {
     "pb": ("psum", [128, 512 * 8], "float32"),
 }
 SEMAPHORES = (["ldw0", "ldw1", "ldg0", "ldg1", "ldx", "zer", "iot", "eye", "sel", "dmm", "gsv", "gsc", "sub0", "sub1", "qv", "qx",
-               "mm0", "mm1", "ev0", "ev1", "st", "hc0", "hc1", "hp", "sent"] + ["arr%d" % j for j in range(N)])
+               "mm0", "mm1", "ev0", "ev1", "st", "sent"] + ["h" + p for p in PIECES]
+              + ["%s_%d" % (p, j) for j in range(N) for p in PIECES])
 
 
 def _bits(m):
     return bin(m).count("1")
+
+
+def _parts(piece):
+    return [piece + "0", piece + "1"] if len(piece) == 1 else [piece]
 
 
 def _roles(s, T, topo):
@@ -48,23 +56,23 @@ def _roles(s, T, topo):
     for i, p in enumerate(T.cores[j] for j in away if topo.same_plane(s, T.cores[j])):
         who["P%d" % i] = p
         who["Q%d" % i] = [T.cores[j] for j in away if topo.mates(T.cores[j], p)][0]
-    able = [c for c in range(256) if c != s and (topo.host(c), topo.chip(c)) == (topo.host(s), topo.chip(s))
-            and all(topo.may_write(c, T.cores[j]) for j in away)]
-    who["far0"], who["far1"] = [c for c in able if topo.die(c) != topo.die(s)][:2]
-    who["near"] = [c for c in able if topo.die(c) == topo.die(s)][0]
+    here = [c for c in range(256) if c != s and (topo.host(c), topo.chip(c)) == (topo.host(s), topo.chip(s))]
+    able = [c for c in here if all(topo.may_write(c, T.cores[j]) for j in away)]
+    who["t0"], who["t1"] = [c for c in able if topo.die(c) != topo.die(s)][:2]
+    who["u0"], who["u1"] = [c for c in here if c not in able and topo.die(c) == topo.die(s)][:2]
     return who
 
 
 def _masks(topo, who):
     off = topo.mask(who["S"], who["M"])
-    return off, topo.mask(who["S"], who["near"]) & ~off
+    return off, topo.mask(who["S"], who["u0"]) & ~off
 
 
 def _view(T, r, piece):
+    a, b = PIECES[piece]
     k = BC * r
-    if piece == "p":
-        return T.vp[:, k:k + BC]
-    a, b = {"c": (0, BC), "c0": (0, NC), "c1": (NC, BC)}[piece]
+    if piece[0] == "p":
+        return T.vp[:, k + a:k + b]
     return T.vq[:, k + a:k + b].bitcast(dt.uint8)
 
 
@@ -85,21 +93,18 @@ def _send(g, core, T, topo, view, *ways):
     return sum(_bits(w[1]) for w in ways)
 
 
-def _writes(name):
-    return (sum(name in dests for piece, feed, dests in OWN)
-            + sum(name in dests for h in HELPERS for piece, dests in HELP[h]))
+def _came(name):
+    return ([piece for piece, feed, dests in OWN if name in dests]
+            + [piece for h in sorted(HELP) for piece, dests in HELP[h] if name in dests])
 
 
 def _helper(g, core, T, topo, s, who, name):
     r = T.rank_of(s)
     off, on = _masks(topo, who)
-    n, seen = 0, []
+    n = 0
     for piece, dests in HELP[name]:
-        for q in ["c0", "c1"] if piece == "c" else [piece]:
-            if q not in seen:
-                seen.append(q)
-                g.wait_ge(T.sem["h" + q], _bits(on))
-        n += _send(g, core, T, topo, _view(T, r, piece), ([who[d] for d in dests], off, T.sem["arr%d" % r]))
+        g.wait_ge(T.sem["h" + piece], _bits(on))
+        n += _send(g, core, T, topo, _view(T, r, piece), ([who[d] for d in dests], off, T.sem["%s_%d" % (piece, r)]))
     g.wait_ge(T.sem.sent, n)
 
 
@@ -109,14 +114,13 @@ def rank_program(g, core, T, topo):
         for s in T.cores:
             if (topo.host(s), topo.chip(s)) == (topo.host(core), topo.chip(core)):
                 who = _roles(s, T, topo)
-                for name in HELPERS:
+                for name in sorted(HELP):
                     if who[name] == core:
                         _helper(g, core, T, topo, s, who, name)
         return
     S = T.sem
     v, t, sc, sy = g.vector, g.tensor, g.scalar, g.sync
     who = _roles(core, T, topo)
-    order = [T.rank_of(who[n]) for n in ORDER]
 
     sy.dma_start(T.wcs[:, 0:NC].bitcast(dt.uint8), T.wc[:, 0:W4]).then_inc(S.ldw0, 16)
     sc.dma_start(T.wps[:], T.ws[:]).then_inc(S.ldw0, 16)
@@ -171,48 +175,49 @@ def rank_program(g, core, T, topo):
     v.quantize_mx(T.xq[:], T.xp[:], T.xt[:]).then_inc(S.qx, 1)
 
     off, on = _masks(topo, who)
-    arr = T.sem["arr%d" % rank]
     n, made = 0, 0
     for piece, feed, dests in OWN:
-        need = 1 if piece == "c0" else WT
+        need = 1 if _parts(piece)[-1][-1] == "0" else WT
         if need > made:
             g.wait_ge(S.qv, need)
             made = need
-        ways = [([who[h] for h in HELPERS], on, T.sem["h" + piece])] if feed else []
+        ways = [([who[h] for h in feed], on, T.sem["h" + piece])] if feed else []
         if dests:
-            ways.append(([who[d] for d in dests], off, arr))
+            ways.append(([who[d] for d in dests], off, T.sem["%s_%d" % (piece, rank)]))
         n += _send(g, core, T, topo, _view(T, rank, piece), *ways)
     g.wait_ge(S.sent, n)
 
     t.wait_ge(S.qv, WT)
     t.wait_ge(S.qx, 1)
-    for i, j in enumerate(order):
+    seen = []
+    for u, (name, h) in enumerate(UNITS):
+        j = T.rank_of(who[name])
         if j != rank:
-            t.wait_ge(T.sem["arr%d" % j], _bits(off) * _writes(ORDER[i]))
-        if i >= 4:
-            t.wait_ge(S.ev0, i - 3)
-            t.wait_ge(S.ev1, i - 3)
-        for h in range(WT):
-            bank = (2 * i + h) % 8
-            k = BC * j + NC * h
-            t.matmul_mx(T.pb[:, 512 * bank:512 * bank + NC], T.vq[:, k:k + NC], T.vp[:, k:k + NC], T.xq[:], T.xp[:],
-                        True, True).then_inc(T.sem["mm%d" % h], 1)
-    for i, j in enumerate(order):
-        b0, b1 = 512 * (2 * i % 8), 512 * ((2 * i + 1) % 8)
-        k = BC * j
-        v.wait_ge(S.mm0, i + 1)
-        v.tensor_copy(T.ys[:, k:k + NC], T.pb[:, b0:b0 + NC]).then_inc(S.ev0, 1)
-        sc.wait_ge(S.mm1, i + 1)
-        sc.activation(T.ys[:, k + NC:k + BC], T.pb[:, b1:b1 + NC], ActivationFunctionType.Copy).then_inc(S.ev1, 1)
+            for q in _came(name):
+                if (j, q) not in seen and set(_parts(q)) & {"c%d" % h, "p%d" % h}:
+                    seen.append((j, q))
+                    t.wait_ge(T.sem["%s_%d" % (q, j)], _bits(off))
+        if u >= 8:
+            t.wait_ge(T.sem["ev%d" % (u % 2)], (u - 8) // 2 + 1)
+        k = BC * j + NC * h
+        b = 512 * (u % 8)
+        t.matmul_mx(T.pb[:, b:b + NC], T.vq[:, k:k + NC], T.vp[:, k:k + NC], T.xq[:], T.xp[:],
+                    True, True).then_inc(T.sem["mm%d" % (u % 2)], 1)
+    for u, (name, h) in enumerate(UNITS):
+        k = BC * T.rank_of(who[name]) + NC * h
+        b = 512 * (u % 8)
+        if u % 2 == 0:
+            v.wait_ge(S.mm0, u // 2 + 1)
+            v.tensor_copy(T.ys[:, k:k + NC], T.pb[:, b:b + NC]).then_inc(S.ev0, 1)
+        else:
+            sc.wait_ge(S.mm1, u // 2 + 1)
+            sc.activation(T.ys[:, k:k + NC], T.pb[:, b:b + NC], ActivationFunctionType.Copy).then_inc(S.ev1, 1)
 
-    for i in [1, 0] + list(range(2, N - 1)):
-        k = BC * order[i]
-        sy.wait_ge(S.ev0, i + 1)
-        sy.wait_ge(S.ev1, i + 1)
-        sy.dma_start(T.y[:, k:k + BC], T.ys[:, k:k + BC]).then_inc(S.st, 16)
-    k = BC * order[N - 1]
-    sy.wait_ge(S.ev0, N)
-    sy.dma_start(T.y[:, k:k + NC], T.ys[:, k:k + NC]).then_inc(S.st, 16)
-    sc.wait_ge(S.ev1, N)
-    sc.dma_start(T.y[:, k + NC:k + BC], T.ys[:, k + NC:k + BC]).then_inc(S.st, 16)
-    sy.wait_ge(S.st, 16 * (N + 1))
+    todo = [(BC * T.rank_of(who[name]), BC, [u for u in range(N * WT) if UNITS[u][0] == name]) for name in WHOLE]
+    todo += [(BC * T.rank_of(who[name]) + NC * h, NC, [u]) for u, (name, h) in enumerate(UNITS) if name not in WHOLE]
+    for i, (k, w, us) in enumerate(todo):
+        q = sc if i == len(todo) - 1 else sy
+        for u in us:
+            q.wait_ge(T.sem["ev%d" % (u % 2)], u // 2 + 1)
+        q.dma_start(T.y[:, k:k + w], T.ys[:, k:k + w]).then_inc(S.st, 16)
+    sy.wait_ge(S.st, 16 * len(todo))

from concourse.bass import DstId, RemoteDMATransfer
from concourse.mybir import dt, AluOpType, ActivationFunctionType

N, WT, NC = 8, 2, 128
BC = WT * NC
W4 = 4 * NC
PIECES = {"c": (0, BC), "c0": (0, NC), "c1": (NC, BC), "p": (0, BC), "p0": (0, NC), "p1": (NC, BC)}

HELP = {
    "t0": [("c0", ["Q0", "Q1", "P1"]), ("p1", ["Q1", "P1"])],
    "t1": [("p0", ["Q1", "P1"]), ("c1", ["Q1", "P1"])],
    "u0": [("c0", ["P2", "P0"]), ("p1", ["P2", "P0"])],
    "u1": [("p0", ["P2", "P0"]), ("c1", ["P2", "P0"])],
}
OWN = [("c0", ["t0", "u0"], []), ("p0", ["t1", "u1"], []), ("c", [], ["Q2"]), ("c1", ["t1", "u1"], ["Q0"]),
       ("p", [], ["Q2", "Q0", "M"]), ("p1", ["t0", "u0"], []), ("c0", [], ["M"]), ("c1", [], ["M"])]
UNITS = [("S", 0), ("S", 1), ("Q2", 0), ("Q2", 1), ("Q0", 1), ("Q0", 0), ("M", 0), ("P2", 0), ("Q1", 0), ("M", 1), ("P0", 0), ("P1", 0),
         ("P2", 1), ("Q1", 1), ("P0", 1), ("P1", 1)]
WHOLE = ["Q2", "S"]

SCRATCH = {
    "wcs": ("sbuf", [128, BC], "float8_e4m3fn_x4"),
    "wps": ("sbuf", [128, BC], "uint8"),
    "gt": ("sbuf", [128, 4 * BC], "bfloat16"),
    "gs": ("sbuf", [128, 4 * BC], "bfloat16"),
    "vt": ("sbuf", [128, 4 * BC], "bfloat16"),
    "xt": ("sbuf", [128, W4], "bfloat16"),
    "et": ("sbuf", [128, NC], "bfloat16"),
    "em": ("sbuf", [128, W4 + 4], "bfloat16"),
    "sq": ("sbuf", [128, W4], "float8_e4m3fn_x4"),
    "sp": ("sbuf", [128, W4], "uint8"),
    "xq": ("sbuf", [128, NC], "float8_e4m3fn_x4"),
    "xp": ("sbuf", [128, NC], "uint8"),
    "vq": ("sbuf", [128, N * BC], "float8_e4m3fn_x4"),
    "vp": ("sbuf", [128, N * BC], "uint8"),
    "ys": ("sbuf", [128, N * BC], "float32"),
    "pb": ("psum", [128, 512 * 8], "float32"),
}
SEMAPHORES = (["ldw0", "ldw1", "ldg0", "ldg1", "ldx", "zer", "iot", "eye", "sel", "dmm", "gsv", "gsc", "sub0", "sub1", "qv", "qx",
               "mm0", "mm1", "ev0", "ev1", "st", "sent"] + ["h" + p for p in PIECES]
              + ["%s_%d" % (p, j) for j in range(N) for p in PIECES])


def _bits(m):
    return bin(m).count("1")


def _parts(piece):
    return [piece + "0", piece + "1"] if len(piece) == 1 else [piece]


def _roles(s, T, topo):
    r = T.rank_of(s)
    away = sorted((j for j in range(N) if j != r), key=lambda j: j ^ r)
    who = {"S": s, "M": [T.cores[j] for j in away if topo.mates(s, T.cores[j])][0]}
    for i, p in enumerate(T.cores[j] for j in away if topo.same_plane(s, T.cores[j])):
        who["P%d" % i] = p
        who["Q%d" % i] = [T.cores[j] for j in away if topo.mates(T.cores[j], p)][0]
    here = [c for c in range(256) if c != s and (topo.host(c), topo.chip(c)) == (topo.host(s), topo.chip(s))]
    able = [c for c in here if all(topo.may_write(c, T.cores[j]) for j in away)]
    who["t0"], who["t1"] = [c for c in able if topo.die(c) != topo.die(s)][:2]
    who["u0"], who["u1"] = [c for c in here if c not in able and topo.die(c) == topo.die(s)][:2]
    return who


def _masks(topo, who):
    off = topo.mask(who["S"], who["M"])
    return off, topo.mask(who["S"], who["u0"]) & ~off


def _view(T, r, piece):
    a, b = PIECES[piece]
    k = BC * r
    if piece[0] == "p":
        return T.vp[:, k + a:k + b]
    return T.vq[:, k + a:k + b].bitcast(dt.uint8)


def _send(g, core, T, topo, view, *ways):
    if len(ways) == 1 and len(ways[0][0]) == 1:
        (d,), mask, sem = ways[0]
        rid, pid = topo.addr(d, core)
        g.remote_dma(out_ap=view, in_ap=view, remote_sem=sem, local_sem=T.sem.sent, pid=pid, routing_id=rid, dma_engine_mask=mask)
        return _bits(mask)
    moves = []
    for dests, mask, sem in ways:
        ids = []
        for d in dests:
            rid, pid = topo.addr(d, core)
            ids.append(DstId(rid=rid, pnc=pid))
        moves.append(RemoteDMATransfer(dst_ids=ids, dma_engine_mask=mask, remote_sem=sem, srcs=[view], dsts=[view for d in dests]))
    g.remote_dma_fused(moves, local_sem=T.sem.sent)
    return sum(_bits(w[1]) for w in ways)


def _came(name):
    return ([piece for piece, feed, dests in OWN if name in dests]
            + [piece for h in sorted(HELP) for piece, dests in HELP[h] if name in dests])


def _helper(g, core, T, topo, s, who, name):
    r = T.rank_of(s)
    off, on = _masks(topo, who)
    n = 0
    for piece, dests in HELP[name]:
        g.wait_ge(T.sem["h" + piece], _bits(on))
        n += _send(g, core, T, topo, _view(T, r, piece), ([who[d] for d in dests], off, T.sem["%s_%d" % (piece, r)]))
    g.wait_ge(T.sem.sent, n)


def rank_program(g, core, T, topo):
    rank = T.rank_of(core)
    if rank is None:
        for s in T.cores:
            if (topo.host(s), topo.chip(s)) == (topo.host(core), topo.chip(core)):
                who = _roles(s, T, topo)
                for name in sorted(HELP):
                    if who[name] == core:
                        _helper(g, core, T, topo, s, who, name)
        return
    S = T.sem
    v, t, sc, sy = g.vector, g.tensor, g.scalar, g.sync
    who = _roles(core, T, topo)

    sy.dma_start(T.wcs[:, 0:NC].bitcast(dt.uint8), T.wc[:, 0:W4]).then_inc(S.ldw0, 16)
    sc.dma_start(T.wps[:], T.ws[:]).then_inc(S.ldw0, 16)
    sc.dma_start(T.gt[:, 0:W4], T.gr[:, 0:W4]).then_inc(S.ldg0, 16)
    sy.dma_start(T.wcs[:, NC:BC].bitcast(dt.uint8), T.wc[:, W4:2 * W4]).then_inc(S.ldw1, 16)
    sy.dma_start(T.gt[:, W4:2 * W4], T.gr[:, W4:2 * W4]).then_inc(S.ldg1, 16)
    sy.wait_ge(S.ldg0, 16)
    sy.dma_start(T.xt[:], T.x[:]).then_inc(S.ldx, 16)

    v.memset(T.em[:], 0.0).then_inc(S.zer, 1)
    g.iota(T.et[:], [[1, NC]], 0, -1, allow_small_or_imprecise_dtypes=True).then_inc(S.iot, 1)
    v.wait_ge(S.iot, 1)
    v.wait_ge(S.zer, 1)
    v.tensor_scalar(T.em[:, 3:W4 + 3:4], T.et[:], 0.0, None, AluOpType.is_equal).then_inc(S.eye, 1)
    v.wait_ge(S.eye, 1)
    for b in range(4):
        v.quantize_mx(T.sq[:, NC * b:NC * b + NC], T.sp[:, NC * b:NC * b + NC], T.em[:, 3 - b:3 - b + W4]).then_inc(S.sel, 1)

    for i in range(WT):
        t.wait_ge(T.sem["ldw%d" % i], 16 * (WT - i))
        for b in range(4):
            if i == 0:
                t.wait_ge(S.sel, b + 1)
            k = 512 * (4 * i + b)
            t.matmul_mx(T.pb[:, k:k + NC], T.sq[:, NC * b:NC * b + NC], T.sp[:, NC * b:NC * b + NC],
                        T.wcs[:, NC * i:NC * i + NC], T.wps[:, NC * i:NC * i + NC], True, True).then_inc(S.dmm, 1)

    v.wait_ge(S.ldg0, 16)
    v.tensor_scalar(T.gs[:, 0:NC], T.gt[:, 0:W4:4], 0.25, None, AluOpType.mult).then_inc(S.gsv, 1)
    for i in range(WT):
        sc.wait_ge(T.sem["ldg%d" % i], 16)
        for b in range(1 - i, 4):
            k = W4 * i
            sc.activation(T.gs[:, k + NC * b:k + NC * b + NC], T.gt[:, k + b:k + W4:4], ActivationFunctionType.Copy,
                          scale=0.25).then_inc(S.gsc, 1)

    for i in range(WT):
        o = W4 * i
        for b in range(4):
            k = 512 * (4 * i + b)
            if i == b == 0:
                v.wait_ge(S.gsv, 1)
            else:
                v.wait_ge(S.gsc, 4 * i + b)
            v.wait_ge(S.dmm, 4 * i + b + 1)
            v.tensor_tensor(T.vt[:, o + b:o + W4:4], T.pb[:, k:k + NC], T.gs[:, o + NC * b:o + NC * b + NC],
                            AluOpType.subtract).then_inc(T.sem["sub%d" % i], 1)
        v.wait_ge(T.sem["sub%d" % i], 4)
        k = BC * rank + NC * i
        v.quantize_mx(T.vq[:, k:k + NC], T.vp[:, k:k + NC], T.vt[:, o:o + W4]).then_inc(S.qv, 1)
    v.wait_ge(S.ldx, 16)
    v.quantize_mx(T.xq[:], T.xp[:], T.xt[:]).then_inc(S.qx, 1)

    off, on = _masks(topo, who)
    n, made = 0, 0
    for piece, feed, dests in OWN:
        need = 1 if _parts(piece)[-1][-1] == "0" else WT
        if need > made:
            g.wait_ge(S.qv, need)
            made = need
        ways = [([who[h] for h in feed], on, T.sem["h" + piece])] if feed else []
        if dests:
            ways.append(([who[d] for d in dests], off, T.sem["%s_%d" % (piece, rank)]))
        n += _send(g, core, T, topo, _view(T, rank, piece), *ways)
    g.wait_ge(S.sent, n)

    t.wait_ge(S.qv, WT)
    t.wait_ge(S.qx, 1)
    seen = []
    for u, (name, h) in enumerate(UNITS):
        j = T.rank_of(who[name])
        if j != rank:
            for q in _came(name):
                if (j, q) not in seen and set(_parts(q)) & {"c%d" % h, "p%d" % h}:
                    seen.append((j, q))
                    t.wait_ge(T.sem["%s_%d" % (q, j)], _bits(off))
        if u >= 8:
            t.wait_ge(T.sem["ev%d" % (u % 2)], (u - 8) // 2 + 1)
        k = BC * j + NC * h
        b = 512 * (u % 8)
        t.matmul_mx(T.pb[:, b:b + NC], T.vq[:, k:k + NC], T.vp[:, k:k + NC], T.xq[:], T.xp[:],
                    True, True).then_inc(T.sem["mm%d" % (u % 2)], 1)
    for u, (name, h) in enumerate(UNITS):
        k = BC * T.rank_of(who[name]) + NC * h
        b = 512 * (u % 8)
        if u % 2 == 0:
            v.wait_ge(S.mm0, u // 2 + 1)
            v.tensor_copy(T.ys[:, k:k + NC], T.pb[:, b:b + NC]).then_inc(S.ev0, 1)
        else:
            sc.wait_ge(S.mm1, u // 2 + 1)
            sc.activation(T.ys[:, k:k + NC], T.pb[:, b:b + NC], ActivationFunctionType.Copy).then_inc(S.ev1, 1)

    todo = [(BC * T.rank_of(who[name]), BC, [u for u in range(N * WT) if UNITS[u][0] == name]) for name in WHOLE]
    todo += [(BC * T.rank_of(who[name]) + NC * h, NC, [u]) for u, (name, h) in enumerate(UNITS) if name not in WHOLE]
    for i, (k, w, us) in enumerate(todo):
        q = sc if i == len(todo) - 1 else sy
        for u in us:
            q.wait_ge(T.sem["ev%d" % (u % 2)], u // 2 + 1)
        q.dma_start(T.y[:, k:k + w], T.ys[:, k:k + w]).then_inc(S.st, 16)
    sy.wait_ge(S.st, 16 * len(todo))
